import numpy as np
import ml_dtypes


def mxq(x, axis, fmt="e4m3"):
    dtype, down = {"e4m3": (ml_dtypes.float8_e4m3fn, 7), "e5m2": (ml_dtypes.float8_e5m2, 14)}[fmt]
    v = np.moveaxis(np.asarray(x, np.float32).astype(ml_dtypes.bfloat16).astype(np.float64), axis, -1)
    blocks = v.reshape(v.shape[:-1] + (-1, 32))
    amax = np.abs(blocks).max(-1, keepdims=True)
    byte = np.maximum(np.where(amax > 0, np.frexp(amax)[1] - 1 + 127, 0) - down, 1)
    scale = np.exp2(byte - 127.0)
    codes = (blocks / scale).astype(np.float32).astype(dtype).astype(np.float64)
    return np.moveaxis((codes * scale).reshape(v.shape), -1, axis)


WIDE = False


def mx_kscale(k):
    if not WIDE:
        return np.ones(k)
    levels = np.array([10, -10, 5, -5, 0])
    if k % 512:
        return np.exp2(np.random.permutation(np.resize(levels, k // 32))).repeat(32)
    a = np.empty((k // 512, 16))
    for p in range(k // 512):
        a[p, :8] = np.random.permutation(np.resize(levels, 8))
        for g in range(8):
            far = levels[np.abs(levels - a[p, g]) >= 10]
            a[p, g + 8] = far[np.random.randint(len(far))]
    return np.exp2(a.ravel()).repeat(32)


def f64(x):
    return np.asarray(x).astype(np.float64)


def striped(idx):
    return np.tile(idx.reshape(-1, 16).T, (8, 1)).astype(np.uint16)


def unstriped(offs):
    return offs[:16].T.reshape(-1).astype(np.int64)


def pack_weight(w):
    k, n = w.shape
    w = f64(np.asarray(w, np.float32).astype(ml_dtypes.bfloat16)).reshape(k // 32, 32, n)
    amax = np.abs(w).max(1)
    byte = np.clip(np.where(amax > 0, np.frexp(amax)[1] - 1 + 127 - 7, 1), 1, 254)
    scaled = (w * np.exp2(127.0 - byte)[:, None, :]).reshape(k, n).astype(np.float32)
    words = np.ascontiguousarray(scaled.reshape(k // 512, 128, 4, n).transpose(0, 1, 3, 2)).astype(ml_dtypes.float8_e4m3fn).view(np.uint8)
    return words, np.ascontiguousarray(byte.astype(np.uint8).reshape(k // 512, 16, n))


def unpack_weight(words, scales):
    g, p, n, _ = words.shape
    vals = np.ascontiguousarray(words).view(ml_dtypes.float8_e4m3fn).astype(np.float64) * np.repeat(np.exp2(scales.astype(np.float64) - 127.0), 8, axis=1)[..., None]
    return vals.transpose(0, 1, 3, 2).reshape(g * 512, n)


K, T, S, N, H, U = 1024, 2048, 512, 256, 512, 1024


def setup_inputs():
    n = np.random.standard_normal
    s = mx_kscale(K)[:, None]
    u = mx_kscale(H)
    packed_xT = pack_weight(n((K, T)) * s)
    return {
        "x_words": packed_xT[0],
        "x_scales": packed_xT[1],
        "w1": (n((K, H)) / np.sqrt(K) / s).astype(np.float32),
        "w2": (n((K, H)) / np.sqrt(K) / s).astype(np.float32),
        "ext": (0.6 * n((H, U))).astype(np.float32),
        "unit": (np.random.uniform(0.6, 1.4, (H, 1)) * u[:, None]).astype(np.float32),
        "w3": (n((H, N)) / np.sqrt(H) / u[:, None]).astype(np.float32),
        "offs": striped(np.random.permutation(T)[:S]),
        "hl": striped(np.random.permutation(np.concatenate([np.arange(S), np.random.randint(0, S, U - S)]))),
        "wt": striped(np.random.permutation(np.concatenate([np.arange(S), np.random.randint(0, S, U - S)]))),
    }


def reference(x_words, x_scales, w1, w2, ext, unit, w3, offs, hl, wt):
    xq = unpack_weight(x_words, x_scales)[:, unstriped(offs)]
    y = mxq(f64(w1), 0, "e4m3").T @ xq
    yh = y[:, unstriped(hl)]
    till = yh + f64(ext)
    z1 = mxq(f64(w2), 0, "e4m3").T @ xq
    zh = z1[:, unstriped(hl)]
    vald = np.minimum(till, zh)
    yw = y[:, unstriped(wt)]
    hid = f64(unit) * (vald * yw)
    return mxq(f64(w3), 0, "e4m3").T @ mxq(hid, 0, "e4m3")

@@ -1,0 +1,203 @@
+from contextlib import ExitStack
+
+import concourse.mybir as mybir
+
+K, T, S, N, H, U = 1024, 2048, 512, 256, 512, 1024
+FLOPS = 2 * (2 * K * H * S + H * N * U)
+
+F32 = mybir.dt.float32
+BF16 = mybir.dt.bfloat16
+I32 = mybir.dt.int32
+U32 = mybir.dt.uint32
+U16 = mybir.dt.uint16
+U8 = mybir.dt.uint8
+FP8X4 = mybir.dt.float8_e4m3fn_x4
+ALU = mybir.AluOpType
+COPY = mybir.ActivationFunctionType.Copy
+
+P = 128
+PACK = 4
+PASSES = K // (P * PACK)
+CHUNKS = [(0, 256), (256, 256), (512, 256), (768, 256)]
+EXT_LOADS = [(0, 256), (256, 256), (512, 512)]
+
+
+def tile_picked_yleaseq_mul_p_kernel(
+    tc, x_words, x_scales, w1, w2, ext, unit, w3, offs, hl, wt, out
+):
+    nc = tc.nc
+    with ExitStack() as ctx:
+        keep = ctx.enter_context(tc.tile_pool(name="keep", bufs=1))
+        work = ctx.enter_context(tc.tile_pool(name="work", bufs=2))
+        psum = ctx.enter_context(tc.psum_pool(name="psum", bufs=1))
+
+        offs_sb = keep.tile([P, S // 16], U16, name="offs_sb")
+        hl_sb = keep.tile([P, U // 16], U16, name="hl_sb")
+        wt_sb = keep.tile([P, U // 16], U16, name="wt_sb")
+        unit_sb = keep.tile([P, PACK], F32, name="unit_sb")
+        xs_all = keep.tile([P, T], U8, name="xs_all", align_bytes=64)
+        xw_all = [keep.tile([P, T], U32, name=f"xw_all{g}", align_bytes=64) for g in range(PASSES)]
+        raw = {}
+        for name in ("w1", "w2"):
+            for g in range(PASSES):
+                raw[name, g] = keep.tile([P, PACK, H], F32, name=f"{name}_raw{g}", align_bytes=64)
+        w3_raw = keep.tile([P, PACK, N], F32, name="w3_raw", align_bytes=64)
+        ext_sb = [keep.tile([P, PACK, n], F32, name=f"ext{r0}", align_bytes=64) for r0, n in EXT_LOADS]
+
+        def load_w(name, w, g):
+            rows = w[g * P * PACK : (g + 1) * P * PACK, :]
+            nc.sync.dma_start(out=raw[name, g][:], in_=rows.rearrange("(p j) c -> p j c", j=PACK))
+
+        def load_x(g):
+            nc.sync.dma_start(
+                out=xw_all[g][:].bitcast(I32), in_=x_words[g].rearrange("p n t -> p (n t)").bitcast(I32)
+            )
+
+        def load_ext(i):
+            r0, n = EXT_LOADS[i]
+            nc.sync.dma_start(out=ext_sb[i][:], in_=ext.rearrange("(p t) r -> p t r", t=PACK)[:, :, r0 : r0 + n])
+
+        nc.gpsimd.memset(xs_all[:].bitcast(I32), 0)
+        nc.sync.dma_start(offs_sb[:], offs)
+        for q in range(4):
+            nc.gpsimd.dma_start(
+                out=xs_all[32 * q : 32 * q + 4 * PASSES, :].bitcast(I32),
+                in_=x_scales[:, 4 * q : 4 * q + 4, :].bitcast(I32),
+            )
+        load_w("w1", w1, 0)
+        load_x(0)
+        load_w("w1", w1, 1)
+        load_x(1)
+        nc.sync.dma_start(out=unit_sb[:], in_=unit.rearrange("(p t) o -> p (t o)", t=PACK))
+        nc.sync.dma_start(wt_sb[:], wt)
+        nc.sync.dma_start(hl_sb[:], hl)
+        load_w("w2", w2, 0)
+        load_w("w2", w2, 1)
+        load_ext(0)
+        load_ext(1)
+        nc.sync.dma_start(out=w3_raw[:], in_=w3.rearrange("(p j) c -> p j c", j=PACK))
+        load_ext(2)
+
+        codes, scales = {}, {}
+
+        def round_w(name, g, copy):
+            grouped = keep.tile([P, PACK, P, PACK], BF16, name=f"{name}_grouped{g}", align_bytes=64)
+            copy(
+                out=grouped[:].rearrange("p t m j -> p m j t"),
+                in_=raw[name, g][:].rearrange("p j (m t) -> p m j t", t=PACK),
+            )
+            return grouped
+
+        def quantize(key, grouped, width):
+            codes[key] = keep.tile([P, width], U32, name=f"codes_{key[0]}{key[1]}", align_bytes=64)
+            scales[key] = keep.tile([P, width], U8, name=f"scales_{key[0]}{key[1]}", align_bytes=64)
+            nc.vector.quantize_mx(out=codes[key][:].bitcast(FP8X4), scales=scales[key][:], in_=grouped)
+
+        def quantize_w(name, g, grouped):
+            quantize((name, g), grouped[:].rearrange("p t m j -> p (t m j)"), H)
+
+        xw = [keep.tile([P, S], U32, name=f"xw{g}", align_bytes=64) for g in range(PASSES)]
+        xs = keep.tile([P, S], U8, name="xs", align_bytes=64)
+
+        def project(name, g, banks):
+            for t in range(PACK):
+                cols = slice(t * P, (t + 1) * P)
+                nc.tensor.matmul_mx(
+                    out=banks[t][:],
+                    lhsT=codes[name, g][:, cols].bitcast(FP8X4),
+                    lhsT_scale=scales[name, g][:, cols],
+                    rhs=xw[g][:].bitcast(FP8X4),
+                    rhs_scale=xs[4 * g : P, :],
+                    start=(g == 0),
+                    stop=(g == PASSES - 1),
+                )
+
+        y_banks = [psum.tile([P, S], F32, name=f"y_bank{t}", tag=f"bank{t}") for t in range(PACK)]
+        z_banks = [psum.tile([P, S], F32, name=f"z_bank{t}", tag=f"bank{PACK + t}") for t in range(PACK)]
+
+        nc.vector.tensor_copy(xs[:], xs_all[:].indirect(offs_sb[:]))
+        for g in range(PASSES):
+            grouped = round_w("w1", g, nc.scalar.copy)
+            nc.vector.tensor_copy(xw[g][:], xw_all[g][:].indirect(offs_sb[:]))
+            quantize_w("w1", g, grouped)
+            project("w1", g, y_banks)
+
+        y = [keep.tile([P, S], F32, name=f"y{t}", align_bytes=64) for t in range(PACK)]
+        yu = [keep.tile([P, S], F32, name=f"yu{t}", align_bytes=64) for t in range(PACK)]
+        z = [keep.tile([P, S], F32, name=f"z{t}", align_bytes=64) for t in range(PACK)]
+
+        grouped = round_w("w2", 0, nc.vector.tensor_copy)
+        for t in range(PACK):
+            nc.scalar.copy(out=y[t][:], in_=y_banks[t][:])
+            nc.vector.tensor_scalar(
+                out=yu[t][:], in0=y[t][:], scalar1=unit_sb[:, t : t + 1], scalar2=None, op0=ALU.mult
+            )
+        quantize_w("w2", 0, grouped)
+        project("w2", 0, z_banks)
+        grouped = round_w("w2", 1, nc.vector.tensor_copy)
+        quantize_w("w2", 1, grouped)
+        project("w2", 1, z_banks)
+
+        def list_cols(r0, n):
+            return slice(r0 // 16, (r0 + n) // 16)
+
+        def fetch(tag, windows, offsets, r0, n):
+            got = work.tile([P, PACK, n], F32, name=tag, tag=tag, align_bytes=64)
+            for t in range(PACK):
+                nc.scalar.activation(got[:, t, :], windows[t][:].indirect(offsets[:, list_cols(r0, n)]), COPY)
+            return got
+
+        def extend(r0, n):
+            till = work.tile([P, PACK, n], F32, name="till", tag="till", align_bytes=64)
+            i = max(i for i, (e0, en) in enumerate(EXT_LOADS) if e0 <= r0)
+            e0 = r0 - EXT_LOADS[i][0]
+            for t in range(PACK):
+                nc.vector.tensor_tensor(
+                    till[:, t, :], y[t][:].indirect(hl_sb[:, list_cols(r0, n)]), ext_sb[i][:, t, e0 : e0 + n], ALU.add
+                )
+            return till
+
+        waiter = {c: fetch("waiter", yu, wt_sb, *CHUNKS[c]) for c in range(2)}
+        for t in range(PACK):
+            nc.scalar.copy(out=z[t][:], in_=z_banks[t][:])
+        till = {0: extend(*CHUNKS[0])}
+
+        w3_grouped = keep.tile([P, N, PACK], BF16, name="w3_grouped", align_bytes=64)
+        nc.vector.tensor_copy(
+            out=w3_grouped[:].rearrange("p (c i) j -> p c j i", i=4),
+            in_=w3_raw[:].rearrange("p j (c i) -> p c j i", i=4),
+        )
+
+        for c, (r0, n) in enumerate(CHUNKS):
+            cut = fetch("cut", z, hl_sb, r0, n)
+            if c + 1 < len(CHUNKS):
+                till[c + 1] = extend(*CHUNKS[c + 1])
+            if c == 0:
+                quantize(("w3", 0), w3_grouped[:].rearrange("p c j -> p (c j)"), N)
+            vald = work.tile([P, PACK, n], F32, name="vald", tag="vald", align_bytes=64)
+            nc.vector.tensor_tensor(vald[:], till[c][:], cut[:], ALU.min)
+            hid = work.tile([P, n, PACK], BF16, name="hid", tag="hid", align_bytes=64)
+            nc.vector.tensor_tensor(
+                hid[:].rearrange("p (c i) t -> p c t i", i=4),
+                vald[:].rearrange("p t (c i) -> p c t i", i=4),
+                waiter[c][:].rearrange("p t (c i) -> p c t i", i=4),
+                ALU.mult,
+            )
+            if c + 2 < len(CHUNKS):
+                waiter[c + 2] = fetch("waiter", yu, wt_sb, *CHUNKS[c + 2])
+            quantize(("hid", c), hid[:].rearrange("p r t -> p (r t)"), n)
+            bank = psum.tile([P, N // P, n], F32, name=f"out_bank{c}", tag=f"bank{c % PACK}")
+            for b in range(N // P):
+                cols = slice(b * P, (b + 1) * P)
+                nc.tensor.matmul_mx(
+                    out=bank[:, b, :],
+                    lhsT=codes["w3", 0][:, cols].bitcast(FP8X4),
+                    lhsT_scale=scales["w3", 0][:, cols],
+                    rhs=codes["hid", c][:].bitcast(FP8X4),
+                    rhs_scale=scales["hid", c][:],
+                    start=True,
+                    stop=True,
+                )
+            result = work.tile([P, N // P, n], F32, name="result", tag="result", align_bytes=64)
+            nc.scalar.copy(out=result[:], in_=bank[:])
+            nc.sync.dma_start(out=out.rearrange("(b p) r -> p b r", p=P)[:, :, r0 : r0 + n], in_=result[:])

@@ -19,6 +19,7 @@ P = 128
 PACK = 4
 PASSES = K // (P * PACK)
 CHUNKS = [(0, 256), (256, 256), (512, 256), (768, 256)]
+Z_ON_SCALAR = 3
 EXT_LOADS = [(0, 256), (256, 256), (512, 512)]
 
 
@@ -57,25 +58,25 @@ def tile_picked_yleaseq_mul_p_kernel(
             r0, n = EXT_LOADS[i]
             nc.sync.dma_start(out=ext_sb[i][:], in_=ext.rearrange("(p t) r -> p t r", t=PACK)[:, :, r0 : r0 + n])
 
-        nc.gpsimd.memset(xs_all[:].bitcast(I32), 0)
+        nc.vector.memset(xs_all[:].bitcast(I32), 0)
         nc.sync.dma_start(offs_sb[:], offs)
+        load_w("w1", w1, 0)
         for q in range(4):
-            nc.gpsimd.dma_start(
+            nc.sync.dma_start(
                 out=xs_all[32 * q : 32 * q + 4 * PASSES, :].bitcast(I32),
                 in_=x_scales[:, 4 * q : 4 * q + 4, :].bitcast(I32),
             )
-        load_w("w1", w1, 0)
         load_x(0)
         load_w("w1", w1, 1)
         load_x(1)
         nc.sync.dma_start(out=unit_sb[:], in_=unit.rearrange("(p t) o -> p (t o)", t=PACK))
         nc.sync.dma_start(wt_sb[:], wt)
+        nc.sync.dma_start(out=w3_raw[:], in_=w3.rearrange("(p j) c -> p j c", j=PACK))
         nc.sync.dma_start(hl_sb[:], hl)
         load_w("w2", w2, 0)
         load_w("w2", w2, 1)
         load_ext(0)
         load_ext(1)
-        nc.sync.dma_start(out=w3_raw[:], in_=w3.rearrange("(p j) c -> p j c", j=PACK))
         load_ext(2)
 
         codes, scales = {}, {}
@@ -124,31 +125,35 @@ def tile_picked_yleaseq_mul_p_kernel(
 
         y = [keep.tile([P, S], F32, name=f"y{t}", align_bytes=64) for t in range(PACK)]
         yu = [keep.tile([P, S], F32, name=f"yu{t}", align_bytes=64) for t in range(PACK)]
-        z = [keep.tile([P, S], F32, name=f"z{t}", align_bytes=64) for t in range(PACK)]
+        z = [keep.tile([P, S], F32, name=f"z{t}", tag=f"z{t}", align_bytes=64) for t in range(PACK)]
 
-        grouped = round_w("w2", 0, nc.vector.tensor_copy)
+        w3_grouped = keep.tile([P, N, PACK], BF16, name="w3_grouped", align_bytes=64)
+        nc.vector.tensor_copy(
+            out=w3_grouped[:].rearrange("p (c i) j -> p c j i", i=4),
+            in_=w3_raw[:].rearrange("p j (c i) -> p c j i", i=4),
+        )
         for t in range(PACK):
             nc.scalar.copy(out=y[t][:], in_=y_banks[t][:])
             nc.vector.tensor_scalar(
                 out=yu[t][:], in0=y[t][:], scalar1=unit_sb[:, t : t + 1], scalar2=None, op0=ALU.mult
             )
-        quantize_w("w2", 0, grouped)
-        project("w2", 0, z_banks)
-        grouped = round_w("w2", 1, nc.vector.tensor_copy)
-        quantize_w("w2", 1, grouped)
-        project("w2", 1, z_banks)
+        quantize(("w3", 0), w3_grouped[:].rearrange("p c j -> p (c j)"), N)
+        for g in range(PASSES):
+            grouped = round_w("w2", g, nc.vector.tensor_copy)
+            quantize_w("w2", g, grouped)
+            project("w2", g, z_banks)
 
         def list_cols(r0, n):
             return slice(r0 // 16, (r0 + n) // 16)
 
-        def fetch(tag, windows, offsets, r0, n):
-            got = work.tile([P, PACK, n], F32, name=tag, tag=tag, align_bytes=64)
+        def fetch(name, windows, offsets, r0, n):
+            got = keep.tile([P, PACK, n], F32, name=f"{name}{r0}", align_bytes=64)
             for t in range(PACK):
                 nc.scalar.activation(got[:, t, :], windows[t][:].indirect(offsets[:, list_cols(r0, n)]), COPY)
             return got
 
         def extend(r0, n):
-            till = work.tile([P, PACK, n], F32, name="till", tag="till", align_bytes=64)
+            till = keep.tile([P, PACK, n], F32, name=f"till{r0}", align_bytes=64)
             i = max(i for i, (e0, en) in enumerate(EXT_LOADS) if e0 <= r0)
             e0 = r0 - EXT_LOADS[i][0]
             for t in range(PACK):
@@ -157,47 +162,56 @@ def tile_picked_yleaseq_mul_p_kernel(
                 )
             return till
 
-        waiter = {c: fetch("waiter", yu, wt_sb, *CHUNKS[c]) for c in range(2)}
         for t in range(PACK):
-            nc.scalar.copy(out=z[t][:], in_=z_banks[t][:])
-        till = {0: extend(*CHUNKS[0])}
+            copy = nc.vector.tensor_copy if t >= Z_ON_SCALAR else nc.scalar.copy
+            copy(out=z[t][:], in_=z_banks[t][:])
+        waiter = [fetch("waiter", yu, wt_sb, r0, n) for r0, n in CHUNKS]
+        till = [extend(r0, n) for r0, n in CHUNKS]
+        cut = [fetch("cut", z, hl_sb, r0, n) for r0, n in CHUNKS]
 
-        w3_grouped = keep.tile([P, N, PACK], BF16, name="w3_grouped", align_bytes=64)
-        nc.vector.tensor_copy(
-            out=w3_grouped[:].rearrange("p (c i) j -> p c j i", i=4),
-            in_=w3_raw[:].rearrange("p j (c i) -> p c j i", i=4),
-        )
-
+        out_rows = out.rearrange("(b p) r -> p b r", p=P)
+        banks = []
         for c, (r0, n) in enumerate(CHUNKS):
-            cut = fetch("cut", z, hl_sb, r0, n)
-            if c + 1 < len(CHUNKS):
-                till[c + 1] = extend(*CHUNKS[c + 1])
-            if c == 0:
-                quantize(("w3", 0), w3_grouped[:].rearrange("p c j -> p (c j)"), N)
+            half = n // 2
+            halves = [slice(0, half), slice(half, n)]
             vald = work.tile([P, PACK, n], F32, name="vald", tag="vald", align_bytes=64)
-            nc.vector.tensor_tensor(vald[:], till[c][:], cut[:], ALU.min)
             hid = work.tile([P, n, PACK], BF16, name="hid", tag="hid", align_bytes=64)
-            nc.vector.tensor_tensor(
-                hid[:].rearrange("p (c i) t -> p c t i", i=4),
-                vald[:].rearrange("p t (c i) -> p c t i", i=4),
-                waiter[c][:].rearrange("p t (c i) -> p c t i", i=4),
-                ALU.mult,
-            )
-            if c + 2 < len(CHUNKS):
-                waiter[c + 2] = fetch("waiter", yu, wt_sb, *CHUNKS[c + 2])
-            quantize(("hid", c), hid[:].rearrange("p r t -> p (r t)"), n)
-            bank = psum.tile([P, N // P, n], F32, name=f"out_bank{c}", tag=f"bank{c % PACK}")
-            for b in range(N // P):
-                cols = slice(b * P, (b + 1) * P)
-                nc.tensor.matmul_mx(
-                    out=bank[:, b, :],
-                    lhsT=codes["w3", 0][:, cols].bitcast(FP8X4),
-                    lhsT_scale=scales["w3", 0][:, cols],
-                    rhs=codes["hid", c][:].bitcast(FP8X4),
-                    rhs_scale=scales["hid", c][:],
-                    start=True,
-                    stop=True,
+            hid_codes = keep.tile([P, n], U32, name=f"hid_codes{c}", align_bytes=64)
+            hid_scales = keep.tile([P, n], U8, name=f"hid_scales{c}", align_bytes=64)
+            for h in halves:
+                nc.vector.tensor_tensor(vald[:, :, h], till[c][:, :, h], cut[c][:, :, h], ALU.min)
+            for h in halves:
+                nc.vector.tensor_tensor(
+                    hid[:, h, :].rearrange("p (c i) t -> p c t i", i=4),
+                    vald[:, :, h].rearrange("p t (c i) -> p c t i", i=4),
+                    waiter[c][:, :, h].rearrange("p t (c i) -> p c t i", i=4),
+                    ALU.mult,
                 )
-            result = work.tile([P, N // P, n], F32, name="result", tag="result", align_bytes=64)
+            for h in halves:
+                nc.vector.quantize_mx(
+                    out=hid_codes[:, h].bitcast(FP8X4),
+                    scales=hid_scales[:, h],
+                    in_=hid[:, h, :].rearrange("p r t -> p (r t)"),
+                )
+            pieces = halves if c == len(CHUNKS) - 1 else [slice(0, n)]
+            for piece in pieces:
+                width = piece.stop - piece.start
+                bank = psum.tile([P, N // P, width], F32, name=f"out_bank{len(banks)}", tag=f"bank{len(banks)}")
+                for b in range(N // P):
+                    cols = slice(b * P, (b + 1) * P)
+                    nc.tensor.matmul_mx(
+                        out=bank[:, b, :],
+                        lhsT=codes["w3", 0][:, cols].bitcast(FP8X4),
+                        lhsT_scale=scales["w3", 0][:, cols],
+                        rhs=hid_codes[:, piece].bitcast(FP8X4),
+                        rhs_scale=hid_scales[:, piece],
+                        start=True,
+                        stop=True,
+                    )
+                banks.append((bank, r0 + piece.start, width))
+
+        for i, (bank, r0, width) in enumerate(banks):
+            tag = f"z{i}" if i < PACK else f"result{i}"
+            result = keep.tile([P, N // P, width], F32, name=f"result{i}", tag=tag, align_bytes=64)
             nc.scalar.copy(out=result[:], in_=bank[:])
-            nc.sync.dma_start(out=out.rearrange("(b p) r -> p b r", p=P)[:, :, r0 : r0 + n], in_=result[:])
+            nc.sync.dma_start(out=out_rows[:, :, r0 : r0 + width], in_=result[:])

@@ -18,9 +18,11 @@ COPY = mybir.ActivationFunctionType.Copy
 P = 128
 PACK = 4
 PASSES = K // (P * PACK)
-CHUNKS = [(0, 256), (256, 256), (512, 256), (768, 256)]
-Z_ON_SCALAR = 3
-EXT_LOADS = [(0, 256), (256, 256), (512, 512)]
+CHUNKS = [(0, 256), (256, 256), (512, 256), (768, 128), (896, 128)]
+HALF = U // 2
+QUARTER = U // 4
+WIDE = S + 16
+Z_ON_SCALAR = 4
 
 
 def tile_picked_yleaseq_mul_p_kernel(
@@ -41,9 +43,11 @@ def tile_picked_yleaseq_mul_p_kernel(
         raw = {}
         for name in ("w1", "w2"):
             for g in range(PASSES):
-                raw[name, g] = keep.tile([P, PACK, H], F32, name=f"{name}_raw{g}", align_bytes=64)
+                raw[name, g] = keep.tile([P, PACK, H], F32, name=f"{name}_raw{g}", tag=f"{name}_raw{g}", align_bytes=64)
         w3_raw = keep.tile([P, PACK, N], F32, name="w3_raw", align_bytes=64)
-        ext_sb = [keep.tile([P, PACK, n], F32, name=f"ext{r0}", align_bytes=64) for r0, n in EXT_LOADS]
+        ext_sb = {
+            (h, u): keep.tile([P, 2, HALF], F32, name=f"ext{h}{u}", align_bytes=64) for h in range(2) for u in range(2)
+        }
 
         def load_w(name, w, g):
             rows = w[g * P * PACK : (g + 1) * P * PACK, :]
@@ -54,18 +58,18 @@ def tile_picked_yleaseq_mul_p_kernel(
                 out=xw_all[g][:].bitcast(I32), in_=x_words[g].rearrange("p n t -> p (n t)").bitcast(I32)
             )
 
-        def load_ext(i):
-            r0, n = EXT_LOADS[i]
-            nc.sync.dma_start(out=ext_sb[i][:], in_=ext.rearrange("(p t) r -> p t r", t=PACK)[:, :, r0 : r0 + n])
+        def load_ext(h, u):
+            rows = ext.rearrange("(p t) r -> p t r", t=PACK)
+            nc.sync.dma_start(out=ext_sb[h, u][:], in_=rows[:, 2 * u : 2 * u + 2, h * HALF : (h + 1) * HALF])
 
         nc.vector.memset(xs_all[:].bitcast(I32), 0)
-        nc.sync.dma_start(offs_sb[:], offs)
         load_w("w1", w1, 0)
         for q in range(4):
             nc.sync.dma_start(
                 out=xs_all[32 * q : 32 * q + 4 * PASSES, :].bitcast(I32),
                 in_=x_scales[:, 4 * q : 4 * q + 4, :].bitcast(I32),
             )
+        nc.sync.dma_start(offs_sb[:], offs)
         load_x(0)
         load_w("w1", w1, 1)
         load_x(1)
@@ -75,9 +79,9 @@ def tile_picked_yleaseq_mul_p_kernel(
         nc.sync.dma_start(hl_sb[:], hl)
         load_w("w2", w2, 0)
         load_w("w2", w2, 1)
-        load_ext(0)
-        load_ext(1)
-        load_ext(2)
+        for h in range(2):
+            for u in range(2):
+                load_ext(h, u)
 
         codes, scales = {}, {}
 
@@ -90,7 +94,7 @@ def tile_picked_yleaseq_mul_p_kernel(
             return grouped
 
         def quantize(key, grouped, width):
-            codes[key] = keep.tile([P, width], U32, name=f"codes_{key[0]}{key[1]}", align_bytes=64)
+            codes[key] = keep.tile([P, width], U32, name="codes", tag=f"codes_{key[0]}{key[1]}", align_bytes=64)
             scales[key] = keep.tile([P, width], U8, name=f"scales_{key[0]}{key[1]}", align_bytes=64)
             nc.vector.quantize_mx(out=codes[key][:].bitcast(FP8X4), scales=scales[key][:], in_=grouped)
 
@@ -118,13 +122,14 @@ def tile_picked_yleaseq_mul_p_kernel(
 
         nc.vector.tensor_copy(xs[:], xs_all[:].indirect(offs_sb[:]))
         for g in range(PASSES):
-            grouped = round_w("w1", g, nc.scalar.copy)
+            quantize_w("w1", g, round_w("w1", g, nc.vector.tensor_copy))
             nc.vector.tensor_copy(xw[g][:], xw_all[g][:].indirect(offs_sb[:]))
-            quantize_w("w1", g, grouped)
             project("w1", g, y_banks)
 
-        y = [keep.tile([P, S], F32, name=f"y{t}", align_bytes=64) for t in range(PACK)]
+        y = [keep.tile([P, WIDE], F32, name=f"y{t}", align_bytes=64) for t in range(PACK)]
         yu = [keep.tile([P, S], F32, name=f"yu{t}", align_bytes=64) for t in range(PACK)]
+        for window in y:
+            nc.gpsimd.memset(window[:, S:WIDE], 0.0)
         z = [keep.tile([P, S], F32, name=f"z{t}", tag=f"z{t}", align_bytes=64) for t in range(PACK)]
 
         w3_grouped = keep.tile([P, N, PACK], BF16, name="w3_grouped", align_bytes=64)
@@ -133,9 +138,11 @@ def tile_picked_yleaseq_mul_p_kernel(
             in_=w3_raw[:].rearrange("p j (c i) -> p c j i", i=4),
         )
         for t in range(PACK):
-            nc.scalar.copy(out=y[t][:], in_=y_banks[t][:])
+            copy = nc.vector.tensor_copy if t == 1 else nc.scalar.copy
+            copy(out=y[t][:, 0:S], in_=y_banks[t][:])
+        for t in range(PACK):
             nc.vector.tensor_scalar(
-                out=yu[t][:], in0=y[t][:], scalar1=unit_sb[:, t : t + 1], scalar2=None, op0=ALU.mult
+                out=yu[t][:, 0:S], in0=y[t][:, 0:S], scalar1=unit_sb[:, t : t + 1], scalar2=None, op0=ALU.mult
             )
         quantize(("w3", 0), w3_grouped[:].rearrange("p c j -> p (c j)"), N)
         for g in range(PASSES):
@@ -146,72 +153,75 @@ def tile_picked_yleaseq_mul_p_kernel(
         def list_cols(r0, n):
             return slice(r0 // 16, (r0 + n) // 16)
 
-        def fetch(name, windows, offsets, r0, n):
-            got = keep.tile([P, PACK, n], F32, name=f"{name}{r0}", align_bytes=64)
+        def fetch(tag, windows, offsets, r0, n):
+            got = keep.tile([P, PACK, n], F32, name="got", tag=tag, align_bytes=64)
             for t in range(PACK):
                 nc.scalar.activation(got[:, t, :], windows[t][:].indirect(offsets[:, list_cols(r0, n)]), COPY)
             return got
 
-        def extend(r0, n):
-            till = keep.tile([P, PACK, n], F32, name=f"till{r0}", align_bytes=64)
-            i = max(i for i, (e0, en) in enumerate(EXT_LOADS) if e0 <= r0)
-            e0 = r0 - EXT_LOADS[i][0]
+        def extend(h):
+            till = keep.tile([P, PACK, HALF], F32, name=f"till{h}", align_bytes=64)
             for t in range(PACK):
                 nc.vector.tensor_tensor(
-                    till[:, t, :], y[t][:].indirect(hl_sb[:, list_cols(r0, n)]), ext_sb[i][:, t, e0 : e0 + n], ALU.add
+                    till[:, t, :],
+                    y[t][:].indirect(hl_sb[:, list_cols(h * HALF, HALF)]),
+                    ext_sb[h, t // 2][:, t % 2, :],
+                    ALU.add,
                 )
             return till
 
         for t in range(PACK):
             copy = nc.vector.tensor_copy if t >= Z_ON_SCALAR else nc.scalar.copy
             copy(out=z[t][:], in_=z_banks[t][:])
-        waiter = [fetch("waiter", yu, wt_sb, r0, n) for r0, n in CHUNKS]
-        till = [extend(r0, n) for r0, n in CHUNKS]
-        cut = [fetch("cut", z, hl_sb, r0, n) for r0, n in CHUNKS]
+        waiter = [fetch(f"waiter{q}", yu, wt_sb, q * QUARTER, QUARTER) for q in range(3)]
+        till = [extend(h) for h in range(2)]
+        cut = [fetch(f"cut{r0}", z, hl_sb, r0, n) for r0, n in CHUNKS if r0 <= HALF]
+        waiter.append(fetch("codes_w21", yu, wt_sb, 3 * QUARTER, QUARTER))
+        cut.extend(fetch(f"cut{r0}", z, hl_sb, r0, n) for r0, n in CHUNKS if r0 > HALF)
+
+        vald, hid, banks = {}, {}, {}
+
+        def cap(c):
+            r0, n = CHUNKS[c]
+            vald[c] = work.tile([P, PACK, n], F32, name="vald", tag="vald", align_bytes=64)
+            nc.vector.tensor_tensor(vald[c][:], till[r0 // HALF][:, :, r0 % HALF : r0 % HALF + n], cut[c][:], ALU.min)
+
+        def multiply(c):
+            r0, n = CHUNKS[c]
+            hid[c] = work.tile([P, n, PACK], BF16, name="hid", tag="hid", align_bytes=64)
+            nc.vector.tensor_tensor(
+                hid[c][:].rearrange("p (c i) t -> p c t i", i=4),
+                vald[c][:].rearrange("p t (c i) -> p c t i", i=4),
+                waiter[r0 // QUARTER][:, :, r0 % QUARTER : r0 % QUARTER + n].rearrange("p t (c i) -> p c t i", i=4),
+                ALU.mult,
+            )
+
+        def serve(c):
+            r0, n = CHUNKS[c]
+            quantize(("hid", c), hid[c][:].rearrange("p r t -> p (r t)"), n)
+            banks[c] = psum.tile([P, N // P, n], F32, name=f"out_bank{c}", tag=f"bank{c}")
+            for b in range(N // P):
+                cols = slice(b * P, (b + 1) * P)
+                nc.tensor.matmul_mx(
+                    out=banks[c][:, b, :],
+                    lhsT=codes["w3", 0][:, cols].bitcast(FP8X4),
+                    lhsT_scale=scales["w3", 0][:, cols],
+                    rhs=codes["hid", c][:].bitcast(FP8X4),
+                    rhs_scale=scales["hid", c][:],
+                    start=True,
+                    stop=True,
+                )
+
+        cap(0)
+        for c in range(len(CHUNKS)):
+            multiply(c)
+            if c + 1 < len(CHUNKS):
+                cap(c + 1)
+            serve(c)
 
         out_rows = out.rearrange("(b p) r -> p b r", p=P)
-        banks = []
         for c, (r0, n) in enumerate(CHUNKS):
-            half = n // 2
-            halves = [slice(0, half), slice(half, n)]
-            vald = work.tile([P, PACK, n], F32, name="vald", tag="vald", align_bytes=64)
-            hid = work.tile([P, n, PACK], BF16, name="hid", tag="hid", align_bytes=64)
-            hid_codes = keep.tile([P, n], U32, name=f"hid_codes{c}", align_bytes=64)
-            hid_scales = keep.tile([P, n], U8, name=f"hid_scales{c}", align_bytes=64)
-            for h in halves:
-                nc.vector.tensor_tensor(vald[:, :, h], till[c][:, :, h], cut[c][:, :, h], ALU.min)
-            for h in halves:
-                nc.vector.tensor_tensor(
-                    hid[:, h, :].rearrange("p (c i) t -> p c t i", i=4),
-                    vald[:, :, h].rearrange("p t (c i) -> p c t i", i=4),
-                    waiter[c][:, :, h].rearrange("p t (c i) -> p c t i", i=4),
-                    ALU.mult,
-                )
-            for h in halves:
-                nc.vector.quantize_mx(
-                    out=hid_codes[:, h].bitcast(FP8X4),
-                    scales=hid_scales[:, h],
-                    in_=hid[:, h, :].rearrange("p r t -> p (r t)"),
-                )
-            pieces = halves if c == len(CHUNKS) - 1 else [slice(0, n)]
-            for piece in pieces:
-                width = piece.stop - piece.start
-                bank = psum.tile([P, N // P, width], F32, name=f"out_bank{len(banks)}", tag=f"bank{len(banks)}")
-                for b in range(N // P):
-                    cols = slice(b * P, (b + 1) * P)
-                    nc.tensor.matmul_mx(
-                        out=bank[:, b, :],
-                        lhsT=codes["w3", 0][:, cols].bitcast(FP8X4),
-                        lhsT_scale=scales["w3", 0][:, cols],
-                        rhs=hid_codes[:, piece].bitcast(FP8X4),
-                        rhs_scale=hid_scales[:, piece],
-                        start=True,
-                        stop=True,
-                    )
-                banks.append((bank, r0 + piece.start, width))
-
-        for i, (bank, r0, width) in enumerate(banks):
-            tag = f"z{i}" if i < PACK else f"result{i}"
-            result = keep.tile([P, N // P, width], F32, name=f"result{i}", tag=tag, align_bytes=64)
-            nc.scalar.copy(out=result[:], in_=bank[:])
-            nc.sync.dma_start(out=out_rows[:, :, r0 : r0 + width], in_=result[:])
+            tag = f"z{c}" if c < PACK else f"result{c}"
+            result = keep.tile([P, N // P, n], F32, name=f"result{c}", tag=tag, align_bytes=64)
+            nc.scalar.copy(out=result[:], in_=banks[c][:])
+            nc.sync.dma_start(out=out_rows[:, :, r0 : r0 + n], in_=result[:])

from contextlib import ExitStack

import concourse.mybir as mybir

K, T, S, N, H, U = 1024, 2048, 512, 256, 512, 1024
FLOPS = 2 * (2 * K * H * S + H * N * U)

F32 = mybir.dt.float32
BF16 = mybir.dt.bfloat16
I32 = mybir.dt.int32
U32 = mybir.dt.uint32
U16 = mybir.dt.uint16
U8 = mybir.dt.uint8
FP8X4 = mybir.dt.float8_e4m3fn_x4
ALU = mybir.AluOpType
COPY = mybir.ActivationFunctionType.Copy

P = 128
PACK = 4
PASSES = K // (P * PACK)
CHUNKS = [(0, 256), (256, 256), (512, 256), (768, 128), (896, 128)]
HALF = U // 2
QUARTER = U // 4
WIDE = S + 16
Z_ON_SCALAR = 4


def tile_picked_yleaseq_mul_p_kernel(
    tc, x_words, x_scales, w1, w2, ext, unit, w3, offs, hl, wt, out
):
    nc = tc.nc
    with ExitStack() as ctx:
        keep = ctx.enter_context(tc.tile_pool(name="keep", bufs=1))
        work = ctx.enter_context(tc.tile_pool(name="work", bufs=2))
        psum = ctx.enter_context(tc.psum_pool(name="psum", bufs=1))

        offs_sb = keep.tile([P, S // 16], U16, name="offs_sb")
        hl_sb = keep.tile([P, U // 16], U16, name="hl_sb")
        wt_sb = keep.tile([P, U // 16], U16, name="wt_sb")
        unit_sb = keep.tile([P, PACK], F32, name="unit_sb")
        xs_all = keep.tile([P, T], U8, name="xs_all", align_bytes=64)
        xw_all = [keep.tile([P, T], U32, name=f"xw_all{g}", align_bytes=64) for g in range(PASSES)]
        raw = {}
        for name in ("w1", "w2"):
            for g in range(PASSES):
                raw[name, g] = keep.tile([P, PACK, H], F32, name=f"{name}_raw{g}", tag=f"{name}_raw{g}", align_bytes=64)
        w3_raw = keep.tile([P, PACK, N], F32, name="w3_raw", align_bytes=64)
        ext_sb = {
            (h, u): keep.tile([P, 2, HALF], F32, name=f"ext{h}{u}", align_bytes=64) for h in range(2) for u in range(2)
        }

        def load_w(name, w, g):
            rows = w[g * P * PACK : (g + 1) * P * PACK, :]
            nc.sync.dma_start(out=raw[name, g][:], in_=rows.rearrange("(p j) c -> p j c", j=PACK))

        def load_x(g):
            nc.sync.dma_start(
                out=xw_all[g][:].bitcast(I32), in_=x_words[g].rearrange("p n t -> p (n t)").bitcast(I32)
            )

        def load_ext(h, u):
            rows = ext.rearrange("(p t) r -> p t r", t=PACK)
            nc.sync.dma_start(out=ext_sb[h, u][:], in_=rows[:, 2 * u : 2 * u + 2, h * HALF : (h + 1) * HALF])

        nc.vector.memset(xs_all[:].bitcast(I32), 0)
        load_w("w1", w1, 0)
        for q in range(4):
            nc.sync.dma_start(
                out=xs_all[32 * q : 32 * q + 4 * PASSES, :].bitcast(I32),
                in_=x_scales[:, 4 * q : 4 * q + 4, :].bitcast(I32),
            )
        nc.sync.dma_start(offs_sb[:], offs)
        load_x(0)
        load_w("w1", w1, 1)
        load_x(1)
        nc.sync.dma_start(out=unit_sb[:], in_=unit.rearrange("(p t) o -> p (t o)", t=PACK))
        nc.sync.dma_start(wt_sb[:], wt)
        nc.sync.dma_start(out=w3_raw[:], in_=w3.rearrange("(p j) c -> p j c", j=PACK))
        nc.sync.dma_start(hl_sb[:], hl)
        load_w("w2", w2, 0)
        load_w("w2", w2, 1)
        for h in range(2):
            for u in range(2):
                load_ext(h, u)

        codes, scales = {}, {}

        def round_w(name, g, copy):
            grouped = keep.tile([P, PACK, P, PACK], BF16, name=f"{name}_grouped{g}", align_bytes=64)
            copy(
                out=grouped[:].rearrange("p t m j -> p m j t"),
                in_=raw[name, g][:].rearrange("p j (m t) -> p m j t", t=PACK),
            )
            return grouped

        def quantize(key, grouped, width):
            codes[key] = keep.tile([P, width], U32, name="codes", tag=f"codes_{key[0]}{key[1]}", align_bytes=64)
            scales[key] = keep.tile([P, width], U8, name=f"scales_{key[0]}{key[1]}", align_bytes=64)
            nc.vector.quantize_mx(out=codes[key][:].bitcast(FP8X4), scales=scales[key][:], in_=grouped)

        def quantize_w(name, g, grouped):
            quantize((name, g), grouped[:].rearrange("p t m j -> p (t m j)"), H)

        xw = [keep.tile([P, S], U32, name=f"xw{g}", align_bytes=64) for g in range(PASSES)]
        xs = keep.tile([P, S], U8, name="xs", align_bytes=64)

        def project(name, g, banks):
            for t in range(PACK):
                cols = slice(t * P, (t + 1) * P)
                nc.tensor.matmul_mx(
                    out=banks[t][:],
                    lhsT=codes[name, g][:, cols].bitcast(FP8X4),
                    lhsT_scale=scales[name, g][:, cols],
                    rhs=xw[g][:].bitcast(FP8X4),
                    rhs_scale=xs[4 * g : P, :],
                    start=(g == 0),
                    stop=(g == PASSES - 1),
                )

        y_banks = [psum.tile([P, S], F32, name=f"y_bank{t}", tag=f"bank{t}") for t in range(PACK)]
        z_banks = [psum.tile([P, S], F32, name=f"z_bank{t}", tag=f"bank{PACK + t}") for t in range(PACK)]

        nc.vector.tensor_copy(xs[:], xs_all[:].indirect(offs_sb[:]))
        for g in range(PASSES):
            quantize_w("w1", g, round_w("w1", g, nc.vector.tensor_copy))
            nc.vector.tensor_copy(xw[g][:], xw_all[g][:].indirect(offs_sb[:]))
            project("w1", g, y_banks)

        y = [keep.tile([P, WIDE], F32, name=f"y{t}", align_bytes=64) for t in range(PACK)]
        yu = [keep.tile([P, S], F32, name=f"yu{t}", align_bytes=64) for t in range(PACK)]
        for window in y:
            nc.gpsimd.memset(window[:, S:WIDE], 0.0)
        z = [keep.tile([P, S], F32, name=f"z{t}", tag=f"z{t}", align_bytes=64) for t in range(PACK)]

        w3_grouped = keep.tile([P, N, PACK], BF16, name="w3_grouped", align_bytes=64)
        nc.vector.tensor_copy(
            out=w3_grouped[:].rearrange("p (c i) j -> p c j i", i=4),
            in_=w3_raw[:].rearrange("p j (c i) -> p c j i", i=4),
        )
        for t in range(PACK):
            copy = nc.vector.tensor_copy if t == 1 else nc.scalar.copy
            copy(out=y[t][:, 0:S], in_=y_banks[t][:])
        for t in range(PACK):
            nc.vector.tensor_scalar(
                out=yu[t][:, 0:S], in0=y[t][:, 0:S], scalar1=unit_sb[:, t : t + 1], scalar2=None, op0=ALU.mult
            )
        quantize(("w3", 0), w3_grouped[:].rearrange("p c j -> p (c j)"), N)
        for g in range(PASSES):
            grouped = round_w("w2", g, nc.vector.tensor_copy)
            quantize_w("w2", g, grouped)
            project("w2", g, z_banks)

        def list_cols(r0, n):
            return slice(r0 // 16, (r0 + n) // 16)

        def fetch(tag, windows, offsets, r0, n):
            got = keep.tile([P, PACK, n], F32, name="got", tag=tag, align_bytes=64)
            for t in range(PACK):
                nc.scalar.activation(got[:, t, :], windows[t][:].indirect(offsets[:, list_cols(r0, n)]), COPY)
            return got

        def extend(h):
            till = keep.tile([P, PACK, HALF], F32, name=f"till{h}", align_bytes=64)
            for t in range(PACK):
                nc.vector.tensor_tensor(
                    till[:, t, :],
                    y[t][:].indirect(hl_sb[:, list_cols(h * HALF, HALF)]),
                    ext_sb[h, t // 2][:, t % 2, :],
                    ALU.add,
                )
            return till

        for t in range(PACK):
            copy = nc.vector.tensor_copy if t >= Z_ON_SCALAR else nc.scalar.copy
            copy(out=z[t][:], in_=z_banks[t][:])
        waiter = [fetch(f"waiter{q}", yu, wt_sb, q * QUARTER, QUARTER) for q in range(3)]
        till = [extend(h) for h in range(2)]
        cut = [fetch(f"cut{r0}", z, hl_sb, r0, n) for r0, n in CHUNKS if r0 <= HALF]
        waiter.append(fetch("codes_w21", yu, wt_sb, 3 * QUARTER, QUARTER))
        cut.extend(fetch(f"cut{r0}", z, hl_sb, r0, n) for r0, n in CHUNKS if r0 > HALF)

        vald, hid, banks = {}, {}, {}

        def cap(c):
            r0, n = CHUNKS[c]
            vald[c] = work.tile([P, PACK, n], F32, name="vald", tag="vald", align_bytes=64)
            nc.vector.tensor_tensor(vald[c][:], till[r0 // HALF][:, :, r0 % HALF : r0 % HALF + n], cut[c][:], ALU.min)

        def multiply(c):
            r0, n = CHUNKS[c]
            hid[c] = work.tile([P, n, PACK], BF16, name="hid", tag="hid", align_bytes=64)
            nc.vector.tensor_tensor(
                hid[c][:].rearrange("p (c i) t -> p c t i", i=4),
                vald[c][:].rearrange("p t (c i) -> p c t i", i=4),
                waiter[r0 // QUARTER][:, :, r0 % QUARTER : r0 % QUARTER + n].rearrange("p t (c i) -> p c t i", i=4),
                ALU.mult,
            )

        def serve(c):
            r0, n = CHUNKS[c]
            quantize(("hid", c), hid[c][:].rearrange("p r t -> p (r t)"), n)
            banks[c] = psum.tile([P, N // P, n], F32, name=f"out_bank{c}", tag=f"bank{c}")
            for b in range(N // P):
                cols = slice(b * P, (b + 1) * P)
                nc.tensor.matmul_mx(
                    out=banks[c][:, b, :],
                    lhsT=codes["w3", 0][:, cols].bitcast(FP8X4),
                    lhsT_scale=scales["w3", 0][:, cols],
                    rhs=codes["hid", c][:].bitcast(FP8X4),
                    rhs_scale=scales["hid", c][:],
                    start=True,
                    stop=True,
                )

        cap(0)
        for c in range(len(CHUNKS)):
            multiply(c)
            if c + 1 < len(CHUNKS):
                cap(c + 1)
            serve(c)

        out_rows = out.rearrange("(b p) r -> p b r", p=P)
        for c, (r0, n) in enumerate(CHUNKS):
            tag = f"z{c}" if c < PACK else f"result{c}"
            result = keep.tile([P, N // P, n], F32, name=f"result{c}", tag=tag, align_bytes=64)
            nc.scalar.copy(out=result[:], in_=banks[c][:])
            nc.sync.dma_start(out=out_rows[:, :, r0 : r0 + n], in_=result[:])
